import numpy as np
import ml_dtypes


def mxq(x, axis, fmt="e4m3"):
    dtype, down = {"e4m3": (ml_dtypes.float8_e4m3fn, 7), "e5m2": (ml_dtypes.float8_e5m2, 14)}[fmt]
    v = np.moveaxis(np.asarray(x, np.float32).astype(ml_dtypes.bfloat16).astype(np.float64), axis, -1)
    blocks = v.reshape(v.shape[:-1] + (-1, 32))
    amax = np.abs(blocks).max(-1, keepdims=True)
    byte = np.maximum(np.where(amax > 0, np.frexp(amax)[1] - 1 + 127, 0) - down, 1)
    scale = np.exp2(byte - 127.0)
    codes = (blocks / scale).astype(np.float32).astype(dtype).astype(np.float64)
    return np.moveaxis((codes * scale).reshape(v.shape), -1, axis)


WIDE = False


def mx_kscale(k):
    if not WIDE:
        return np.ones(k)
    levels = np.array([10, -10, 5, -5, 0])
    if k % 512:
        return np.exp2(np.random.permutation(np.resize(levels, k // 32))).repeat(32)
    a = np.empty((k // 512, 16))
    for p in range(k // 512):
        a[p, :8] = np.random.permutation(np.resize(levels, 8))
        for g in range(8):
            far = levels[np.abs(levels - a[p, g]) >= 10]
            a[p, g + 8] = far[np.random.randint(len(far))]
    return np.exp2(a.ravel()).repeat(32)


def f64(x):
    return np.asarray(x).astype(np.float64)


def striped8(idx):
    return np.asarray(idx).reshape(8, -1, 16).transpose(0, 2, 1).reshape(128, -1).astype(np.uint16)


def unstriped8(offs):
    return offs.reshape(8, 16, -1).transpose(0, 2, 1).reshape(8, -1).astype(np.int64)


def pick8(x, idx, run):
    r = np.arange(len(x))
    return x[r[:, None], idx[r % (8 * run) // run]]


E2M1 = np.array([0.0, 0.5, 1.0, 1.5, 2.0, 3.0, 4.0, 6.0, -0.0, -0.5, -1.0, -1.5, -2.0, -3.0, -4.0, -6.0])


def pack_weight(w, fmt):
    k, n = w.shape
    w = f64(np.asarray(w, np.float32).astype(ml_dtypes.bfloat16)).reshape(k // 32, 32, n)
    amax = np.abs(w).max(1)
    if fmt == "e4m3":
        byte = np.frexp(amax)[1] - 1 + 127 - 7
    else:
        mant, ex = np.frexp(amax / 6.0)
        byte = np.where(mant > 0.5, ex, ex - 1) + 127
    byte = np.clip(np.where(amax > 0, byte, 1), 1, 254)
    scaled = (w * np.exp2(127.0 - byte)[:, None, :]).reshape(k, n).astype(np.float32)
    by_word = np.ascontiguousarray(scaled.reshape(k // 512, 128, 4, n).transpose(0, 1, 3, 2))
    if fmt == "e4m3":
        words = by_word.astype(ml_dtypes.float8_e4m3fn).view(np.uint8)
    else:
        c = by_word.astype(ml_dtypes.float4_e2m1fn).view(np.uint8) & 0xF
        words = (c[..., 0::2] | (c[..., 1::2] << 4)).reshape(k // 512, 128, 2 * n)
    return np.ascontiguousarray(words), np.ascontiguousarray(byte.astype(np.uint8).reshape(k // 512, 16, n))


def unpack_weight(words, scales, fmt):
    g, _, n = scales.shape
    words = np.ascontiguousarray(words).reshape(g, 128, n, -1)
    if fmt == "e4m3":
        vals = words.view(ml_dtypes.float8_e4m3fn).astype(np.float64)
    else:
        nib = np.empty((g, 128, n, 4), np.uint8)
        nib[..., 0::2] = words & 0xF
        nib[..., 1::2] = words >> 4
        vals = E2M1[nib]
    vals = vals * np.repeat(np.exp2(scales.astype(np.float64) - 127.0), 8, axis=1)[..., None]
    return vals.transpose(0, 1, 3, 2).reshape(g * 512, n)


D, T, U, X, I, J, M, Q = 512, 1024, 1024, 1024, 512, 256, 128, 128


def setup_inputs():
    n = np.random.standard_normal
    idx = np.stack([np.random.permutation(U)[:I] for _ in range(8)])
    idx2 = np.stack([np.random.permutation(T)[:I] for _ in range(8)])
    idx3 = np.stack([np.random.permutation(T)[:J] for _ in range(8)])
    idx4 = np.stack([np.random.permutation(X)[:M] for _ in range(8)])
    idx5 = np.stack([np.random.permutation(U)[:M] for _ in range(8)])
    idx6 = np.stack([np.random.permutation(T)[:I] for _ in range(8)])
    idx7 = np.stack([np.random.permutation(X)[:I] for _ in range(8)])
    idx8 = np.stack([np.random.permutation(U)[:I] for _ in range(8)])
    fd = mx_kscale(D)
    cachep = pack_weight(n((D, T)) / fd[:, None], "e2m1")
    draftp = pack_weight(n((D, U)) / fd[:, None], "e4m3")
    archp = pack_weight(n((D, X)) / fd[:, None], "e2m1")
    return {
        "query": (n((D, Q)) * 1.0 / np.sqrt(D) * fd[:, None]).astype(np.float32),
        "cache_words": cachep[0],
        "cache_scales": cachep[1],
        "draft_words": draftp[0],
        "draft_scales": draftp[1],
        "arch_words": archp[0],
        "arch_scales": archp[1],
        "offs": striped8(idx),
        "offs2": striped8(idx2),
        "offs3": striped8(idx3),
        "offs4": striped8(idx4),
        "offs5": striped8(idx5),
        "offs6": striped8(idx6),
        "offs7": striped8(idx7),
        "offs8": striped8(idx8),
    }


def reference(query, cache_words, cache_scales, draft_words, draft_scales, arch_words, arch_scales, offs, offs2, offs3, offs4, offs5, offs6, offs7, offs8):
    idx = unstriped8(offs)
    idx2 = unstriped8(offs2)
    idx3 = unstriped8(offs3)
    idx4 = unstriped8(offs4)
    idx5 = unstriped8(offs5)
    idx6 = unstriped8(offs6)
    idx7 = unstriped8(offs7)
    idx8 = unstriped8(offs8)
    cacheu = unpack_weight(cache_words, cache_scales, "e2m1")
    draftu = unpack_weight(draft_words, draft_scales, "e4m3")
    archu = unpack_weight(arch_words, arch_scales, "e2m1")
    queryq = mxq(f64(query), 0, "e4m3")
    a = queryq.T @ cacheu
    b = queryq.T @ draftu
    c0 = queryq.T @ archu
    w = pick8(b, idx, 16) - pick8(a, idx2, 16)
    acc = w[:, 0:0 + J]
    rty = w[:, 256:256 + M]
    drp = w[:, 384:384 + M]
    f1 = np.zeros((Q, T))
    f1[np.arange(Q)[:, None], idx3[np.arange(Q) % 128 // 16]] = acc
    f2 = np.zeros((Q, X))
    f2[np.arange(Q)[:, None], idx4[np.arange(Q) % 128 // 16]] = rty
    f3 = np.zeros((Q, U))
    f3[np.arange(Q)[:, None], idx5[np.arange(Q) % 128 // 16]] = drp
    aa = a + f1
    cc = c0 - f2
    bb = b - f3
    v = np.maximum(pick8(aa, idx6, 16), pick8(cc, idx7, 16))
    y = v - pick8(bb, idx8, 16)
    return y

@@ -1,0 +1,170 @@
+from contextlib import ExitStack
+
+import concourse.mybir as mybir
+
+F32 = mybir.dt.float32
+BF16 = mybir.dt.bfloat16
+I32 = mybir.dt.int32
+U32 = mybir.dt.uint32
+U16 = mybir.dt.uint16
+U8 = mybir.dt.uint8
+FP8X4 = mybir.dt.float8_e4m3fn_x4
+FP4X4 = mybir.dt.float4_e2m1fn_x4
+COPY = mybir.ActivationFunctionType.Copy
+ADD = mybir.AluOpType.add
+SUB = mybir.AluOpType.subtract
+MAX = mybir.AluOpType.max
+
+P = 128
+D, T, Q, I, J, M = 512, 1024, 128, 512, 256, 128
+H = 256
+FLOPS = 2 * D * Q * 3 * T
+
+
+def tile_attend_acceptretry_three_kernel(
+    tc, query, cache_words, cache_scales, draft_words, draft_scales, arch_words, arch_scales,
+    offs, offs2, offs3, offs4, offs5, offs6, offs7, offs8, out,
+):
+    nc = tc.nc
+    with ExitStack() as ctx:
+        sb = ctx.enter_context(tc.tile_pool(name="sb", bufs=1))
+        ps = ctx.enter_context(tc.psum_pool(name="ps", bufs=1))
+
+        def load_scales(name, scales):
+            plane = sb.tile([P, 2 * T], U8, name=name, align_bytes=64)
+            words = plane[:].bitcast(I32)
+            rows = scales[0].bitcast(I32)
+            for h in range(2):
+                nc.sync.dma_start(
+                    words[64 * h : 64 * h + 4, :].rearrange("r (q c) -> r q c", q=2),
+                    rows[8 * h : 8 * h + 8, :].rearrange("(q r) c -> r q c", r=4),
+                )
+            for h in range(2):
+                nc.vector.tensor_copy(words[64 * h + 32 : 64 * h + 36, 0 : T // 4], words[64 * h : 64 * h + 4, T // 4 : T // 2])
+            return plane
+
+        def load_scales_direct(name, scales):
+            plane = sb.tile([P, T], U8, name=name, align_bytes=64)
+            words = plane[:].bitcast(I32)
+            rows = scales[0].bitcast(I32)
+            for g in range(4):
+                nc.sync.dma_start(words[32 * g : 32 * g + 4, :], rows[4 * g : 4 * g + 4, :])
+            return plane
+
+        def load_bytes(name, src):
+            t = sb.tile([P, src.shape[1]], U8, name=name, align_bytes=64)
+            nc.sync.dma_start(t[:].bitcast(I32), src.bitcast(I32))
+            return t
+
+        def load_list(name, src):
+            t = sb.tile([P, src.shape[1]], U16, name=name)
+            nc.sync.dma_start(t[:], src)
+            return t
+
+        q_raw = sb.tile([P, 4, Q], F32, name="q_raw")
+        nc.sync.dma_start(q_raw[:], query.rearrange("(p j) q -> p j q", j=4))
+        cache_s = load_scales("cache_s", cache_scales)
+        cache_w = load_bytes("cache_w", cache_words[0])
+        draft_s = load_scales("draft_s", draft_scales)
+        dw = draft_words[0].rearrange("p n t -> p (n t)")
+        draft_w = [load_bytes("draft_w%d" % h, dw[:, 2048 * h : 2048 * (h + 1)]) for h in range(2)]
+        l2 = load_list("l2", offs2)
+        l1 = load_list("l1", offs)
+        l5 = load_list("l5", offs5)
+        l4 = load_list("l4", offs4)
+        l3 = load_list("l3", offs3)
+        arch_s = load_scales_direct("arch_s", arch_scales)
+        arch_w = load_bytes("arch_w", arch_words[0])
+        l8 = load_list("l8", offs8)
+        l7 = load_list("l7", offs7)
+        l6 = load_list("l6", offs6)
+
+        q_bf = sb.tile([P, Q, 4], BF16, name="q_bf", align_bytes=64)
+        nc.vector.tensor_copy(
+            q_bf[:].rearrange("p (c i) t -> p c t i", i=4), q_raw[:].rearrange("p t (c i) -> p c t i", i=4)
+        )
+        q_codes = sb.tile([P, Q], U32, name="q_codes", align_bytes=64)
+        q_scales = sb.tile([P, Q], U8, name="q_scales", align_bytes=64)
+        nc.vector.quantize_mx(q_codes[:].bitcast(FP8X4), q_scales[:], q_bf[:].rearrange("p q t -> p (q t)"))
+
+        f1 = sb.tile([P, T], F32, name="f1")
+        f2 = sb.tile([P, T], F32, name="f2")
+        f3 = sb.tile([P, T], F32, name="f3")
+        for f in (f3, f2, f1):
+            nc.vector.memset(f[:], 0.0)
+
+        def score(name, codes, plane, c0, n):
+            bank = ps.tile([P, n], F32, name=name)
+            nc.tensor.matmul_mx(bank[:], q_codes[:].bitcast(FP8X4), q_scales[:], codes, plane[:, c0 : c0 + n], start=True, stop=True)
+            return bank
+
+        def fp4(words, c0, n):
+            return words[:, 2 * c0 : 2 * (c0 + n)].bitcast(FP4X4)
+
+        def fp8(c0, n):
+            h, r = divmod(c0, 512)
+            return draft_w[h][:, 4 * r : 4 * (r + n)].bitcast(FP8X4)
+
+        a = sb.tile([P, T], F32, name="a")
+        b = sb.tile([P, T], F32, name="b")
+        pa0 = score("pa0", fp4(cache_w, 0, 512), cache_s, 0, 512)
+        pa1 = score("pa1", fp4(cache_w, 512, 256), cache_s, 512, 256)
+        pa2 = score("pa2", fp4(cache_w, 768, 256), cache_s, 768, 256)
+        pb0 = score("pb0", fp8(0, 512), draft_s, 0, 512)
+        pb1 = score("pb1", fp8(512, 256), draft_s, 512, 256)
+        pb2 = score("pb2", fp8(768, 256), draft_s, 768, 256)
+        pc = [score("pc%d" % h, fp4(arch_w, 512 * h, 512), arch_s, 512 * h, 512) for h in range(2)]
+
+        nc.scalar.activation(a[:, 0:512], pa0[:], COPY)
+        nc.vector.tensor_copy(a[:, 512:768], pa1[:])
+        nc.scalar.activation(a[:, 768:1024], pa2[:], COPY)
+
+        ga_hi = sb.tile([P, H], F32, name="ga_hi")
+        ga_lo = sb.tile([P, H], F32, name="ga_lo")
+        nc.vector.tensor_copy(ga_hi[:], a[:].indirect(l2[:, 16:32]))
+        nc.scalar.activation(ga_lo[:], a[:].indirect(l2[:, 0:16]), COPY)
+
+        nc.scalar.activation(b[:, 0:512], pb0[:], COPY)
+        nc.vector.tensor_copy(b[:, 512:768], pb1[:])
+        nc.vector.tensor_copy(b[:, 768:1024], pb2[:])
+
+        w_hi = sb.tile([P, H], F32, name="w_hi")
+        w_lo = sb.tile([P, H], F32, name="w_lo")
+        nc.vector.tensor_tensor(w_hi[:], b[:].indirect(l1[:, 16:32]), ga_hi[:], SUB)
+        nc.vector.tensor_tensor(w_lo[:], b[:].indirect(l1[:, 0:16]), ga_lo[:], SUB)
+
+        nc.scalar.activation(f3[:].indirect(l5[:]), w_hi[:, M : 2 * M], COPY)
+        nc.scalar.activation(f2[:].indirect(l4[:]), w_hi[:, 0:M], COPY)
+        nc.scalar.activation(f1[:].indirect(l3[:]), w_lo[:], COPY)
+
+        aa = sb.tile([P, T], F32, name="aa")
+        bb = sb.tile([P, T], F32, name="bb")
+        cc = sb.tile([P, T], F32, name="cc")
+        nc.vector.tensor_tensor(bb[:], b[:], f3[:], SUB)
+        for h in range(2):
+            nc.vector.tensor_tensor(cc[:, 512 * h : 512 * (h + 1)], pc[h][:], f2[:, 512 * h : 512 * (h + 1)], SUB)
+
+        gb_lo = sb.tile([P, H], F32, name="gb_lo")
+        gb_hi = sb.tile([P, H], F32, name="gb_hi")
+        gc_lo = sb.tile([P, H], F32, name="gc_lo")
+        gc_hi = sb.tile([P, H], F32, name="gc_hi")
+        gaa_hi = sb.tile([P, H], F32, name="gaa_hi")
+        nc.vector.tensor_copy(gb_lo[:], bb[:].indirect(l8[:, 0:16]))
+        nc.vector.tensor_tensor(aa[:], a[:], f1[:], ADD)
+        nc.scalar.activation(gc_lo[:], cc[:].indirect(l7[:, 0:16]), COPY)
+        nc.scalar.activation(gc_hi[:], cc[:].indirect(l7[:, 16:32]), COPY)
+        nc.scalar.activation(gb_hi[:], bb[:].indirect(l8[:, 16:32]), COPY)
+        nc.scalar.activation(gaa_hi[:], aa[:].indirect(l6[:, 16:32]), COPY)
+
+        d_lo = sb.tile([P, H], F32, name="d_lo")
+        e_lo = sb.tile([P, H], F32, name="e_lo")
+        o_lo = sb.tile([P, H], F32, name="o_lo")
+        v_hi = sb.tile([P, H], F32, name="v_hi")
+        o_hi = sb.tile([P, H], F32, name="o_hi")
+        nc.vector.tensor_tensor(d_lo[:], gc_lo[:], gb_lo[:], SUB)
+        nc.vector.tensor_tensor(e_lo[:], aa[:].indirect(l6[:, 0:16]), gb_lo[:], SUB)
+        nc.vector.tensor_tensor(v_hi[:], gaa_hi[:], gc_hi[:], MAX)
+        nc.vector.tensor_tensor(o_lo[:], e_lo[:], d_lo[:], MAX)
+        nc.sync.dma_start(out[:, 0:H], o_lo[:])
+        nc.vector.tensor_tensor(o_hi[:], v_hi[:], gb_hi[:], SUB)
+        nc.sync.dma_start(out[:, H : 2 * H], o_hi[:])

@@ -64,17 +64,17 @@ def tile_attend_acceptretry_three_kernel(
         q_raw = sb.tile([P, 4, Q], F32, name="q_raw")
         nc.sync.dma_start(q_raw[:], query.rearrange("(p j) q -> p j q", j=4))
         cache_s = load_scales("cache_s", cache_scales)
-        cache_w = load_bytes("cache_w", cache_words[0])
         draft_s = load_scales("draft_s", draft_scales)
+        cache_w = load_bytes("cache_w", cache_words[0])
         dw = draft_words[0].rearrange("p n t -> p (n t)")
         draft_w = [load_bytes("draft_w%d" % h, dw[:, 2048 * h : 2048 * (h + 1)]) for h in range(2)]
+        arch_w = load_bytes("arch_w", arch_words[0])
+        arch_s = load_scales_direct("arch_s", arch_scales)
         l2 = load_list("l2", offs2)
         l1 = load_list("l1", offs)
         l5 = load_list("l5", offs5)
         l4 = load_list("l4", offs4)
         l3 = load_list("l3", offs3)
-        arch_s = load_scales_direct("arch_s", arch_scales)
-        arch_w = load_bytes("arch_w", arch_words[0])
         l8 = load_list("l8", offs8)
         l7 = load_list("l7", offs7)
         l6 = load_list("l6", offs6)
@@ -122,11 +122,10 @@ def tile_attend_acceptretry_three_kernel(
         ga_hi = sb.tile([P, H], F32, name="ga_hi")
         ga_lo = sb.tile([P, H], F32, name="ga_lo")
         nc.vector.tensor_copy(ga_hi[:], a[:].indirect(l2[:, 16:32]))
-        nc.scalar.activation(ga_lo[:], a[:].indirect(l2[:, 0:16]), COPY)
-
         nc.scalar.activation(b[:, 0:512], pb0[:], COPY)
-        nc.vector.tensor_copy(b[:, 512:768], pb1[:])
+        nc.scalar.activation(b[:, 512:768], pb1[:], COPY)
         nc.vector.tensor_copy(b[:, 768:1024], pb2[:])
+        nc.scalar.activation(ga_lo[:], a[:].indirect(l2[:, 0:16]), COPY)
 
         w_hi = sb.tile([P, H], F32, name="w_hi")
         w_lo = sb.tile([P, H], F32, name="w_lo")

@@ -30,26 +30,11 @@ def tile_attend_acceptretry_three_kernel(
         sb = ctx.enter_context(tc.tile_pool(name="sb", bufs=1))
         ps = ctx.enter_context(tc.psum_pool(name="ps", bufs=1))
 
-        def load_scales(name, scales):
-            plane = sb.tile([P, 2 * T], U8, name=name, align_bytes=64)
-            words = plane[:].bitcast(I32)
-            rows = scales[0].bitcast(I32)
-            for h in range(2):
-                nc.sync.dma_start(
-                    words[64 * h : 64 * h + 4, :].rearrange("r (q c) -> r q c", q=2),
-                    rows[8 * h : 8 * h + 8, :].rearrange("(q r) c -> r q c", r=4),
-                )
-            for h in range(2):
-                nc.vector.tensor_copy(words[64 * h + 32 : 64 * h + 36, 0 : T // 4], words[64 * h : 64 * h + 4, T // 4 : T // 2])
-            return plane
+        def scale_plane(name):
+            return sb.tile([P, T], U8, name=name, align_bytes=64)
 
-        def load_scales_direct(name, scales):
-            plane = sb.tile([P, T], U8, name=name, align_bytes=64)
-            words = plane[:].bitcast(I32)
-            rows = scales[0].bitcast(I32)
-            for g in range(4):
-                nc.sync.dma_start(words[32 * g : 32 * g + 4, :], rows[4 * g : 4 * g + 4, :])
-            return plane
+        def load_scale_rows(plane, first, scales, r):
+            nc.sync.dma_start(plane[:].bitcast(I32)[first + r : P : 32, :], scales[0].bitcast(I32)[r:16:4, :])
 
         def load_bytes(name, src):
             t = sb.tile([P, src.shape[1]], U8, name=name, align_bytes=64)
@@ -63,16 +48,22 @@ def tile_attend_acceptretry_three_kernel(
 
         q_raw = sb.tile([P, 4, Q], F32, name="q_raw")
         nc.sync.dma_start(q_raw[:], query.rearrange("(p j) q -> p j q", j=4))
-        cache_s = load_scales("cache_s", cache_scales)
-        draft_s = load_scales("draft_s", draft_scales)
+        cache_s = scale_plane("cache_s")
+        draft_s = scale_plane("draft_s")
+        arch_s = scale_plane("arch_s")
+        for r in range(4):
+            load_scale_rows(cache_s, 0, cache_scales, r)
         cache_w = load_bytes("cache_w", cache_words[0])
-        dw = draft_words[0].rearrange("p n t -> p (n t)")
-        draft_w = [load_bytes("draft_w%d" % h, dw[:, 2048 * h : 2048 * (h + 1)]) for h in range(2)]
-        arch_w = load_bytes("arch_w", arch_words[0])
-        arch_s = load_scales_direct("arch_s", arch_scales)
+        draft_w = load_bytes("draft_w", draft_words[0].rearrange("p n t -> p (n t)"))
+        load_scale_rows(draft_s, 4, draft_scales, 0)
+        for r in range(1, 4):
+            load_scale_rows(draft_s, 4, draft_scales, r)
         l2 = load_list("l2", offs2)
         l1 = load_list("l1", offs)
+        arch_w = load_bytes("arch_w", arch_words[0])
         l5 = load_list("l5", offs5)
+        for r in range(4):
+            load_scale_rows(arch_s, 0, arch_scales, r)
         l4 = load_list("l4", offs4)
         l3 = load_list("l3", offs3)
         l8 = load_list("l8", offs8)
@@ -87,11 +78,12 @@ def tile_attend_acceptretry_three_kernel(
         q_scales = sb.tile([P, Q], U8, name="q_scales", align_bytes=64)
         nc.vector.quantize_mx(q_codes[:].bitcast(FP8X4), q_scales[:], q_bf[:].rearrange("p q t -> p (q t)"))
 
-        f1 = sb.tile([P, T], F32, name="f1")
-        f2 = sb.tile([P, T], F32, name="f2")
+        f1 = sb.tile([P, T], F32, name="f1", tag="f1")
+        f2 = sb.tile([P, T], F32, name="f2", tag="f2")
         f3 = sb.tile([P, T], F32, name="f3")
-        for f in (f3, f2, f1):
-            nc.vector.memset(f[:], 0.0)
+        nc.vector.memset(f3[:], 0.0)
+        nc.vector.memset(f2[:], 0.0)
+        nc.gpsimd.memset(f1[:], 0.0)
 
         def score(name, codes, plane, c0, n):
             bank = ps.tile([P, n], F32, name=name)
@@ -102,17 +94,16 @@ def tile_attend_acceptretry_three_kernel(
             return words[:, 2 * c0 : 2 * (c0 + n)].bitcast(FP4X4)
 
         def fp8(c0, n):
-            h, r = divmod(c0, 512)
-            return draft_w[h][:, 4 * r : 4 * (r + n)].bitcast(FP8X4)
+            return draft_w[:, 4 * c0 : 4 * (c0 + n)].bitcast(FP8X4)
 
-        a = sb.tile([P, T], F32, name="a")
+        a = sb.tile([P, T], F32, name="a", tag="a")
         b = sb.tile([P, T], F32, name="b")
         pa0 = score("pa0", fp4(cache_w, 0, 512), cache_s, 0, 512)
         pa1 = score("pa1", fp4(cache_w, 512, 256), cache_s, 512, 256)
         pa2 = score("pa2", fp4(cache_w, 768, 256), cache_s, 768, 256)
-        pb0 = score("pb0", fp8(0, 512), draft_s, 0, 512)
-        pb1 = score("pb1", fp8(512, 256), draft_s, 512, 256)
-        pb2 = score("pb2", fp8(768, 256), draft_s, 768, 256)
+        pb0 = score("pb0", fp8(0, 512), draft_s[4:P, :], 0, 512)
+        pb1 = score("pb1", fp8(512, 256), draft_s[4:P, :], 512, 256)
+        pb2 = score("pb2", fp8(768, 256), draft_s[4:P, :], 768, 256)
         pc = [score("pc%d" % h, fp4(arch_w, 512 * h, 512), arch_s, 512 * h, 512) for h in range(2)]
 
         nc.scalar.activation(a[:, 0:512], pa0[:], COPY)
@@ -136,33 +127,36 @@ def tile_attend_acceptretry_three_kernel(
         nc.scalar.activation(f2[:].indirect(l4[:]), w_hi[:, 0:M], COPY)
         nc.scalar.activation(f1[:].indirect(l3[:]), w_lo[:], COPY)
 
-        aa = sb.tile([P, T], F32, name="aa")
         bb = sb.tile([P, T], F32, name="bb")
         cc = sb.tile([P, T], F32, name="cc")
-        nc.vector.tensor_tensor(bb[:], b[:], f3[:], SUB)
+        nc.gpsimd.tensor_tensor(bb[:, 512:1024], b[:, 512:1024], f3[:, 512:1024], SUB)
+        nc.vector.tensor_tensor(bb[:, 0:512], pb0[:], f3[:, 0:512], SUB)
         for h in range(2):
             nc.vector.tensor_tensor(cc[:, 512 * h : 512 * (h + 1)], pc[h][:], f2[:, 512 * h : 512 * (h + 1)], SUB)
 
+        aa = sb.tile([P, T], F32, name="aa", tag="f2")
         gb_lo = sb.tile([P, H], F32, name="gb_lo")
-        gb_hi = sb.tile([P, H], F32, name="gb_hi")
         gc_lo = sb.tile([P, H], F32, name="gc_lo")
         gc_hi = sb.tile([P, H], F32, name="gc_hi")
         gaa_hi = sb.tile([P, H], F32, name="gaa_hi")
         nc.vector.tensor_copy(gb_lo[:], bb[:].indirect(l8[:, 0:16]))
-        nc.vector.tensor_tensor(aa[:], a[:], f1[:], ADD)
+        nc.gpsimd.tensor_tensor(aa[:, 768:1024], a[:, 768:1024], f1[:, 768:1024], ADD)
+        nc.vector.tensor_tensor(aa[:, 0:512], pa0[:], f1[:, 0:512], ADD)
+        nc.vector.tensor_tensor(aa[:, 512:768], pa1[:], f1[:, 512:768], ADD)
         nc.scalar.activation(gc_lo[:], cc[:].indirect(l7[:, 0:16]), COPY)
         nc.scalar.activation(gc_hi[:], cc[:].indirect(l7[:, 16:32]), COPY)
-        nc.scalar.activation(gb_hi[:], bb[:].indirect(l8[:, 16:32]), COPY)
         nc.scalar.activation(gaa_hi[:], aa[:].indirect(l6[:, 16:32]), COPY)
+        gb_hi = sb.tile([P, H], F32, name="gb_hi", tag="f1")
+        nc.scalar.activation(gb_hi[:], bb[:].indirect(l8[:, 16:32]), COPY)
 
-        d_lo = sb.tile([P, H], F32, name="d_lo")
+        d_lo = sb.tile([P, H], F32, name="d_lo", tag="a")
         e_lo = sb.tile([P, H], F32, name="e_lo")
-        o_lo = sb.tile([P, H], F32, name="o_lo")
         v_hi = sb.tile([P, H], F32, name="v_hi")
         o_hi = sb.tile([P, H], F32, name="o_hi")
-        nc.vector.tensor_tensor(d_lo[:], gc_lo[:], gb_lo[:], SUB)
         nc.vector.tensor_tensor(e_lo[:], aa[:].indirect(l6[:, 0:16]), gb_lo[:], SUB)
+        nc.vector.tensor_tensor(d_lo[:], gc_lo[:], gb_lo[:], SUB)
         nc.vector.tensor_tensor(v_hi[:], gaa_hi[:], gc_hi[:], MAX)
+        o_lo = sb.tile([P, H], F32, name="o_lo")
         nc.vector.tensor_tensor(o_lo[:], e_lo[:], d_lo[:], MAX)
         nc.sync.dma_start(out[:, 0:H], o_lo[:])
         nc.vector.tensor_tensor(o_hi[:], v_hi[:], gb_hi[:], SUB)

from contextlib import ExitStack

import concourse.mybir as mybir

F32 = mybir.dt.float32
BF16 = mybir.dt.bfloat16
I32 = mybir.dt.int32
U32 = mybir.dt.uint32
U16 = mybir.dt.uint16
U8 = mybir.dt.uint8
FP8X4 = mybir.dt.float8_e4m3fn_x4
FP4X4 = mybir.dt.float4_e2m1fn_x4
COPY = mybir.ActivationFunctionType.Copy
ADD = mybir.AluOpType.add
SUB = mybir.AluOpType.subtract
MAX = mybir.AluOpType.max

P = 128
D, T, Q, I, J, M = 512, 1024, 128, 512, 256, 128
H = 256
FLOPS = 2 * D * Q * 3 * T


def tile_attend_acceptretry_three_kernel(
    tc, query, cache_words, cache_scales, draft_words, draft_scales, arch_words, arch_scales,
    offs, offs2, offs3, offs4, offs5, offs6, offs7, offs8, out,
):
    nc = tc.nc
    with ExitStack() as ctx:
        sb = ctx.enter_context(tc.tile_pool(name="sb", bufs=1))
        ps = ctx.enter_context(tc.psum_pool(name="ps", bufs=1))

        def scale_plane(name):
            return sb.tile([P, T], U8, name=name, align_bytes=64)

        def load_scale_rows(plane, first, scales, r):
            nc.sync.dma_start(plane[:].bitcast(I32)[first + r : P : 32, :], scales[0].bitcast(I32)[r:16:4, :])

        def load_bytes(name, src):
            t = sb.tile([P, src.shape[1]], U8, name=name, align_bytes=64)
            nc.sync.dma_start(t[:].bitcast(I32), src.bitcast(I32))
            return t

        def load_list(name, src):
            t = sb.tile([P, src.shape[1]], U16, name=name)
            nc.sync.dma_start(t[:], src)
            return t

        q_raw = sb.tile([P, 4, Q], F32, name="q_raw")
        nc.sync.dma_start(q_raw[:], query.rearrange("(p j) q -> p j q", j=4))
        cache_s = scale_plane("cache_s")
        draft_s = scale_plane("draft_s")
        arch_s = scale_plane("arch_s")
        for r in range(4):
            load_scale_rows(cache_s, 0, cache_scales, r)
        cache_w = load_bytes("cache_w", cache_words[0])
        draft_w = load_bytes("draft_w", draft_words[0].rearrange("p n t -> p (n t)"))
        load_scale_rows(draft_s, 4, draft_scales, 0)
        for r in range(1, 4):
            load_scale_rows(draft_s, 4, draft_scales, r)
        l2 = load_list("l2", offs2)
        l1 = load_list("l1", offs)
        arch_w = load_bytes("arch_w", arch_words[0])
        l5 = load_list("l5", offs5)
        for r in range(4):
            load_scale_rows(arch_s, 0, arch_scales, r)
        l4 = load_list("l4", offs4)
        l3 = load_list("l3", offs3)
        l8 = load_list("l8", offs8)
        l7 = load_list("l7", offs7)
        l6 = load_list("l6", offs6)

        q_bf = sb.tile([P, Q, 4], BF16, name="q_bf", align_bytes=64)
        nc.vector.tensor_copy(
            q_bf[:].rearrange("p (c i) t -> p c t i", i=4), q_raw[:].rearrange("p t (c i) -> p c t i", i=4)
        )
        q_codes = sb.tile([P, Q], U32, name="q_codes", align_bytes=64)
        q_scales = sb.tile([P, Q], U8, name="q_scales", align_bytes=64)
        nc.vector.quantize_mx(q_codes[:].bitcast(FP8X4), q_scales[:], q_bf[:].rearrange("p q t -> p (q t)"))

        f1 = sb.tile([P, T], F32, name="f1", tag="f1")
        f2 = sb.tile([P, T], F32, name="f2", tag="f2")
        f3 = sb.tile([P, T], F32, name="f3")
        nc.vector.memset(f3[:], 0.0)
        nc.vector.memset(f2[:], 0.0)
        nc.gpsimd.memset(f1[:], 0.0)

        def score(name, codes, plane, c0, n):
            bank = ps.tile([P, n], F32, name=name)
            nc.tensor.matmul_mx(bank[:], q_codes[:].bitcast(FP8X4), q_scales[:], codes, plane[:, c0 : c0 + n], start=True, stop=True)
            return bank

        def fp4(words, c0, n):
            return words[:, 2 * c0 : 2 * (c0 + n)].bitcast(FP4X4)

        def fp8(c0, n):
            return draft_w[:, 4 * c0 : 4 * (c0 + n)].bitcast(FP8X4)

        a = sb.tile([P, T], F32, name="a", tag="a")
        b = sb.tile([P, T], F32, name="b")
        pa0 = score("pa0", fp4(cache_w, 0, 512), cache_s, 0, 512)
        pa1 = score("pa1", fp4(cache_w, 512, 256), cache_s, 512, 256)
        pa2 = score("pa2", fp4(cache_w, 768, 256), cache_s, 768, 256)
        pb0 = score("pb0", fp8(0, 512), draft_s[4:P, :], 0, 512)
        pb1 = score("pb1", fp8(512, 256), draft_s[4:P, :], 512, 256)
        pb2 = score("pb2", fp8(768, 256), draft_s[4:P, :], 768, 256)
        pc = [score("pc%d" % h, fp4(arch_w, 512 * h, 512), arch_s, 512 * h, 512) for h in range(2)]

        nc.scalar.activation(a[:, 0:512], pa0[:], COPY)
        nc.vector.tensor_copy(a[:, 512:768], pa1[:])
        nc.scalar.activation(a[:, 768:1024], pa2[:], COPY)

        ga_hi = sb.tile([P, H], F32, name="ga_hi")
        ga_lo = sb.tile([P, H], F32, name="ga_lo")
        nc.vector.tensor_copy(ga_hi[:], a[:].indirect(l2[:, 16:32]))
        nc.scalar.activation(b[:, 0:512], pb0[:], COPY)
        nc.scalar.activation(b[:, 512:768], pb1[:], COPY)
        nc.vector.tensor_copy(b[:, 768:1024], pb2[:])
        nc.scalar.activation(ga_lo[:], a[:].indirect(l2[:, 0:16]), COPY)

        w_hi = sb.tile([P, H], F32, name="w_hi")
        w_lo = sb.tile([P, H], F32, name="w_lo")
        nc.vector.tensor_tensor(w_hi[:], b[:].indirect(l1[:, 16:32]), ga_hi[:], SUB)
        nc.vector.tensor_tensor(w_lo[:], b[:].indirect(l1[:, 0:16]), ga_lo[:], SUB)

        nc.scalar.activation(f3[:].indirect(l5[:]), w_hi[:, M : 2 * M], COPY)
        nc.scalar.activation(f2[:].indirect(l4[:]), w_hi[:, 0:M], COPY)
        nc.scalar.activation(f1[:].indirect(l3[:]), w_lo[:], COPY)

        bb = sb.tile([P, T], F32, name="bb")
        cc = sb.tile([P, T], F32, name="cc")
        nc.gpsimd.tensor_tensor(bb[:, 512:1024], b[:, 512:1024], f3[:, 512:1024], SUB)
        nc.vector.tensor_tensor(bb[:, 0:512], pb0[:], f3[:, 0:512], SUB)
        for h in range(2):
            nc.vector.tensor_tensor(cc[:, 512 * h : 512 * (h + 1)], pc[h][:], f2[:, 512 * h : 512 * (h + 1)], SUB)

        aa = sb.tile([P, T], F32, name="aa", tag="f2")
        gb_lo = sb.tile([P, H], F32, name="gb_lo")
        gc_lo = sb.tile([P, H], F32, name="gc_lo")
        gc_hi = sb.tile([P, H], F32, name="gc_hi")
        gaa_hi = sb.tile([P, H], F32, name="gaa_hi")
        nc.vector.tensor_copy(gb_lo[:], bb[:].indirect(l8[:, 0:16]))
        nc.gpsimd.tensor_tensor(aa[:, 768:1024], a[:, 768:1024], f1[:, 768:1024], ADD)
        nc.vector.tensor_tensor(aa[:, 0:512], pa0[:], f1[:, 0:512], ADD)
        nc.vector.tensor_tensor(aa[:, 512:768], pa1[:], f1[:, 512:768], ADD)
        nc.scalar.activation(gc_lo[:], cc[:].indirect(l7[:, 0:16]), COPY)
        nc.scalar.activation(gc_hi[:], cc[:].indirect(l7[:, 16:32]), COPY)
        nc.scalar.activation(gaa_hi[:], aa[:].indirect(l6[:, 16:32]), COPY)
        gb_hi = sb.tile([P, H], F32, name="gb_hi", tag="f1")
        nc.scalar.activation(gb_hi[:], bb[:].indirect(l8[:, 16:32]), COPY)

        d_lo = sb.tile([P, H], F32, name="d_lo", tag="a")
        e_lo = sb.tile([P, H], F32, name="e_lo")
        v_hi = sb.tile([P, H], F32, name="v_hi")
        o_hi = sb.tile([P, H], F32, name="o_hi")
        nc.vector.tensor_tensor(e_lo[:], aa[:].indirect(l6[:, 0:16]), gb_lo[:], SUB)
        nc.vector.tensor_tensor(d_lo[:], gc_lo[:], gb_lo[:], SUB)
        nc.vector.tensor_tensor(v_hi[:], gaa_hi[:], gc_hi[:], MAX)
        o_lo = sb.tile([P, H], F32, name="o_lo")
        nc.vector.tensor_tensor(o_lo[:], e_lo[:], d_lo[:], MAX)
        nc.sync.dma_start(out[:, 0:H], o_lo[:])
        nc.vector.tensor_tensor(o_hi[:], v_hi[:], gb_hi[:], SUB)
        nc.sync.dma_start(out[:, H : 2 * H], o_hi[:])
